import numpy as np
import ml_dtypes


def mxq(x, axis, fmt="e4m3"):
    dtype, down = {"e4m3": (ml_dtypes.float8_e4m3fn, 7), "e5m2": (ml_dtypes.float8_e5m2, 14)}[fmt]
    v = np.moveaxis(np.asarray(x, np.float32).astype(ml_dtypes.bfloat16).astype(np.float64), axis, -1)
    blocks = v.reshape(v.shape[:-1] + (-1, 32))
    amax = np.abs(blocks).max(-1, keepdims=True)
    byte = np.maximum(np.where(amax > 0, np.frexp(amax)[1] - 1 + 127, 0) - down, 1)
    scale = np.exp2(byte - 127.0)
    codes = (blocks / scale).astype(np.float32).astype(dtype).astype(np.float64)
    return np.moveaxis((codes * scale).reshape(v.shape), -1, axis)


WIDE = False


def mx_kscale(k):
    if not WIDE:
        return np.ones(k)
    levels = np.array([10, -10, 5, -5, 0])
    if k % 512:
        return np.exp2(np.random.permutation(np.resize(levels, k // 32))).repeat(32)
    a = np.empty((k // 512, 16))
    for p in range(k // 512):
        a[p, :8] = np.random.permutation(np.resize(levels, 8))
        for g in range(8):
            far = levels[np.abs(levels - a[p, g]) >= 10]
            a[p, g + 8] = far[np.random.randint(len(far))]
    return np.exp2(a.ravel()).repeat(32)


def f64(x):
    return np.asarray(x).astype(np.float64)


def striped(idx):
    return np.tile(idx.reshape(-1, 16).T, (8, 1)).astype(np.uint16)


def unstriped(offs):
    return offs[:16].T.reshape(-1).astype(np.int64)


def pack_weight(w):
    k, n = w.shape
    w = f64(np.asarray(w, np.float32).astype(ml_dtypes.bfloat16)).reshape(k // 32, 32, n)
    amax = np.abs(w).max(1)
    byte = np.clip(np.where(amax > 0, np.frexp(amax)[1] - 1 + 127 - 7, 1), 1, 254)
    scaled = (w * np.exp2(127.0 - byte)[:, None, :]).reshape(k, n).astype(np.float32)
    words = np.ascontiguousarray(scaled.reshape(k // 512, 128, 4, n).transpose(0, 1, 3, 2)).astype(ml_dtypes.float8_e4m3fn).view(np.uint8)
    return words, np.ascontiguousarray(byte.astype(np.uint8).reshape(k // 512, 16, n))


def unpack_weight(words, scales):
    g, p, n, _ = words.shape
    vals = np.ascontiguousarray(words).view(ml_dtypes.float8_e4m3fn).astype(np.float64) * np.repeat(np.exp2(scales.astype(np.float64) - 127.0), 8, axis=1)[..., None]
    return vals.transpose(0, 1, 3, 2).reshape(g * 512, n)


def sigmoid(v):
    return 1.0 / (1.0 + np.exp(-np.maximum(v, -700.0)))


K, T, S, N, H = 512, 2048, 512, 128, 512


def setup_inputs():
    n = np.random.standard_normal
    s = mx_kscale(K)[:, None]
    u = mx_kscale(H)
    packed_xT = pack_weight(n((K, T)) * s)
    return {
        "x_words": packed_xT[0],
        "x_scales": packed_xT[1],
        "w1": (n((K, H)) / np.sqrt(K) / s).astype(np.float32),
        "w2": (n((K, H)) / np.sqrt(K) / s).astype(np.float32),
        "unit": (np.random.uniform(0.6, 1.4, (H, 1)) * u[:, None]).astype(np.float32),
        "w3": (n((H, N)) / np.sqrt(H) / u[:, None]).astype(np.float32),
        "offs": striped(np.random.permutation(T)[:S]),
        "s1": striped(np.random.permutation(S)),
        "s2": striped(np.random.permutation(S)),
        "far": striped(np.random.permutation(S)),
    }


def reference(x_words, x_scales, w1, w2, unit, w3, offs, s1, s2, far):
    xq = unpack_weight(x_words, x_scales)[:, unstriped(offs)]
    ys = mxq(f64(w2), 0, "e4m3").T @ xq
    crest = sigmoid(ys)
    y = mxq(f64(w1), 0, "e4m3").T @ xq
    inten = np.exp(0.8 * np.tanh(y))
    ia = inten[:, unstriped(s1)]
    ib = inten[:, unstriped(s2)]
    sur = 0.5 * (ia + ib)
    r1 = np.log(inten) - np.log(sur)
    if_ = inten[:, unstriped(far)]
    r2 = np.log(inten) - np.log(if_)
    msr = crest * r1 + (-1.0 * crest + 1.0) * r2
    hid = f64(unit) * msr
    return mxq(f64(w3), 0, "e4m3").T @ mxq(hid, 0, "e4m3")

@@ -1,0 +1,193 @@
+from contextlib import ExitStack
+
+import concourse.mybir as mybir
+
+K, T, S, N, H = 512, 2048, 512, 128, 512
+FLOPS = 2 * K * H * S * 2 + 2 * H * N * S
+
+F32 = mybir.dt.float32
+BF16 = mybir.dt.bfloat16
+I32 = mybir.dt.int32
+U32 = mybir.dt.uint32
+U16 = mybir.dt.uint16
+U8 = mybir.dt.uint8
+FP8X4 = mybir.dt.float8_e4m3fn_x4
+ACT = mybir.ActivationFunctionType
+ALU = mybir.AluOpType
+
+P = 128
+PACK = 4
+SPARE = 16
+CHUNKS = (256, 128, 128)
+
+
+def tile_picked_yretnx_msr_p_kernel(
+    tc, x_words, x_scales, w1, w2, unit, w3, offs, s1, s2, far, out
+):
+    nc = tc.nc
+    with ExitStack() as ctx:
+        keep = ctx.enter_context(tc.tile_pool(name="keep", bufs=1))
+        psum = ctx.enter_context(tc.psum_pool(name="psum", bufs=1))
+
+        def tile(name, shape, dtype):
+            return keep.tile(shape, dtype, name=name, align_bytes=64)
+
+        w1_raw = tile("w1_raw", [P, PACK, H], F32)
+        nc.sync.dma_start(out=w1_raw[:], in_=w1.rearrange("(p j) c -> p j c", j=PACK))
+        offs_sb = tile("offs_sb", [P, S // 16], U16)
+        nc.sync.dma_start(offs_sb[:], offs)
+        xs_all = tile("xs_all", [P, T], U8)
+        nc.vector.memset(xs_all[:].bitcast(I32), 0)
+        for q in range(4):
+            nc.scalar.dma_start(
+                out=xs_all[32 * q : 32 * q + 4, :].bitcast(I32),
+                in_=x_scales[0, 4 * q : 4 * q + 4, :].bitcast(I32),
+            )
+        xw_all = tile("xw_all", [P, T], U32)
+        nc.sync.dma_start(
+            out=xw_all[:].bitcast(I32),
+            in_=x_words[0].rearrange("p n t -> p (n t)").bitcast(I32),
+        )
+        w2_raw = tile("w2_raw", [P, PACK, H], F32)
+        nc.sync.dma_start(out=w2_raw[:], in_=w2.rearrange("(p j) c -> p j c", j=PACK))
+        s1_sb = tile("s1_sb", [P, S // 16], U16)
+        nc.sync.dma_start(s1_sb[:], s1)
+        s2_sb = tile("s2_sb", [P, S // 16], U16)
+        nc.sync.dma_start(s2_sb[:], s2)
+        far_sb = tile("far_sb", [P, S // 16], U16)
+        nc.sync.dma_start(far_sb[:], far)
+        unit_sb = tile("unit_sb", [P, PACK], F32)
+        nc.sync.dma_start(out=unit_sb[:], in_=unit.rearrange("(p t) o -> p (t o)", t=PACK))
+        w3_raw = tile("w3_raw", [P, PACK, N], F32)
+        nc.sync.dma_start(out=w3_raw[:], in_=w3.rearrange("(p j) n -> p j n", j=PACK))
+
+        def copy(on_scalar, dst, src):
+            if on_scalar:
+                nc.scalar.copy(out=dst, in_=src)
+            else:
+                nc.vector.tensor_copy(out=dst, in_=src)
+
+        def deal(raw, name, engines):
+            grouped = tile(name + "_bf", [P, PACK, P, PACK], BF16)
+            dst = grouped[:].rearrange("p t m j -> p m j t")
+            src = raw[:].rearrange("p j (m t) -> p m j t", t=PACK)
+            share = P // len(engines)
+            for e, on_scalar in enumerate(engines):
+                copy(on_scalar, dst[:, e * share : (e + 1) * share], src[:, e * share : (e + 1) * share])
+            return grouped[:].rearrange("p t m j -> p (t m j)")
+
+        def quantize(src, name, width):
+            codes = tile(name + "_codes", [P, width], U32)
+            scales = tile(name + "_scales", [P, width], U8)
+            nc.vector.quantize_mx(out=codes[:].bitcast(FP8X4), scales=scales[:], in_=src)
+            return codes, scales
+
+        w1_codes, w1_scales = quantize(deal(w1_raw, "w1", (False, True)), "w1", H)
+
+        xs = tile("xs", [P, S], U8)
+        nc.vector.tensor_copy(xs[:], xs_all[:].indirect(offs_sb[:]))
+        xw = tile("xw", [P, S], U32)
+        nc.vector.tensor_copy(xw[:], xw_all[:].indirect(offs_sb[:]))
+
+        def product(bank, codes, scales, t):
+            cols = slice(t * P, (t + 1) * P)
+            nc.tensor.matmul_mx(
+                out=bank[:],
+                lhsT=codes[:, cols].bitcast(FP8X4),
+                lhsT_scale=scales[:, cols],
+                rhs=xw[:].bitcast(FP8X4),
+                rhs_scale=xs[:],
+                start=True,
+                stop=True,
+            )
+
+        y = [psum.tile([P, S], F32, name="y%d" % t, tag="bank%d" % t) for t in range(PACK)]
+        for t in range(PACK):
+            product(y[t], w1_codes, w1_scales, t)
+
+        w2_codes, w2_scales = quantize(deal(w2_raw, "w2", (False,)), "w2", H)
+        ys = [psum.tile([P, S], F32, name="ys%d" % t, tag="bank%d" % (PACK + t)) for t in range(PACK)]
+        for t in range(PACK):
+            product(ys[t], w2_codes, w2_scales, t)
+
+        u8 = tile("u8", [P, PACK], F32)
+        u4 = tile("u4", [P, PACK], F32)
+        u5 = tile("u5", [P, PACK], F32)
+        for dst, factor in ((u8, 0.8), (u4, 0.4), (u5, 0.5)):
+            nc.gpsimd.tensor_scalar(dst[:], unit_sb[:], factor, 0.0, ALU.mult, ALU.add)
+
+        th = [tile("th%d" % t, [P, 2 * S], F32) for t in range(PACK)]
+        inten = [tile("inten%d" % t, [P, S + SPARE], F32) for t in range(PACK)]
+        for t in range(PACK):
+            nc.gpsimd.memset(inten[t][:, S:], 0.0)
+        near = tile("near", [P, PACK, S], F32)
+        both = tile("both", [P, PACK, S], F32)
+        far_w = tile("far_w", [P, PACK, S], F32)
+        far_term = tile("far_term", [P, PACK, S], F32)
+        part = tile("part", [P, PACK, S], F32)
+        near_w = tile("near_w", [P, PACK, S], F32)
+        log_sur = tile("log_sur", [P, PACK, S], F32)
+        near_term = tile("near_term", [P, PACK, S], F32)
+
+        def surround(t):
+            nc.scalar.activation(th[t][:, :S], y[t][:], ACT.Tanh)
+            nc.scalar.activation(inten[t][:, :S], th[t][:, :S], ACT.Exp, scale=0.8)
+            nc.scalar.activation(near[:, t, :], inten[t][:].indirect(s1_sb[:]), ACT.Copy)
+            nc.vector.tensor_tensor(both[:, t, :], inten[t][:].indirect(s2_sb[:]), near[:, t, :], ALU.add)
+
+        def mixing(t):
+            nc.scalar.activation(th[t][:, S:], ys[t][:], ACT.Tanh, scale=0.5)
+            nc.vector.tensor_scalar(far_w[:, t, :], th[t][:, S:], -1.0, u4[:, t : t + 1], ALU.add, ALU.mult)
+
+        def far_side(t):
+            nc.vector.tensor_tensor(far_term[:, t, :], th[t][:].indirect(far_sb[:]), far_w[:, t, :], ALU.mult)
+            nc.vector.scalar_tensor_tensor(
+                part[:, t, :], th[t][:, :S], u8[:, t : t + 1], far_term[:, t, :], ALU.mult, ALU.add
+            )
+
+        surround(0)
+        for t in range(PACK):
+            mixing(t)
+            if t + 1 < PACK:
+                surround(t + 1)
+            far_side(t)
+
+        w3_bf = tile("w3_bf", [P, N, PACK], BF16)
+        nc.scalar.copy(
+            out=w3_bf[:].rearrange("p (c i) j -> p c j i", i=4),
+            in_=w3_raw[:].rearrange("p j (c i) -> p c j i", i=4),
+        )
+        w3_codes, w3_scales = quantize(w3_bf[:].rearrange("p n j -> p (n j)"), "w3", N)
+
+        for t in range(PACK):
+            nc.scalar.activation(
+                near_w[:, t, :], th[t][:, S:], ACT.Identity, bias=u5[:, t : t + 1], scale=u5[:, t : t + 1]
+            )
+
+        c0 = 0
+        for n, width in enumerate(CHUNKS):
+            cols = slice(c0, c0 + width)
+            c0 += width
+            nc.scalar.activation(log_sur[:, :, cols], both[:, :, cols], ACT.Ln, scale=0.5)
+            nc.vector.tensor_tensor(near_term[:, :, cols], near_w[:, :, cols], log_sur[:, :, cols], ALU.mult)
+            hid = tile("hid%d" % n, [P, width, PACK], BF16)
+            nc.vector.tensor_tensor(
+                hid[:].rearrange("p (c i) t -> p c t i", i=4),
+                part[:, :, cols].rearrange("p t (c i) -> p c t i", i=4),
+                near_term[:, :, cols].rearrange("p t (c i) -> p c t i", i=4),
+                ALU.subtract,
+            )
+            hid_codes, hid_scales = quantize(hid[:].rearrange("p c t -> p (c t)"), "hid%d" % n, width)
+            acc = psum.tile([P, width], F32, name="acc%d" % n, tag="bank%d" % n)
+            nc.tensor.matmul_mx(
+                out=acc[:],
+                lhsT=w3_codes[:].bitcast(FP8X4),
+                lhsT_scale=w3_scales[:],
+                rhs=hid_codes[:].bitcast(FP8X4),
+                rhs_scale=hid_scales[:],
+                start=True,
+                stop=True,
+            )
+            res = tile("res%d" % n, [P, width], F32)
+            nc.scalar.copy(out=res[:], in_=acc[:])
+            nc.sync.dma_start(out=out[:, cols], in_=res[:])

@@ -19,6 +19,7 @@ P = 128
 PACK = 4
 SPARE = 16
 CHUNKS = (256, 128, 128)
+HALF = S // 2
 
 
 def tile_picked_yretnx_msr_p_kernel(
@@ -29,20 +30,26 @@ def tile_picked_yretnx_msr_p_kernel(
         keep = ctx.enter_context(tc.tile_pool(name="keep", bufs=1))
         psum = ctx.enter_context(tc.psum_pool(name="psum", bufs=1))
 
-        def tile(name, shape, dtype):
-            return keep.tile(shape, dtype, name=name, align_bytes=64)
+        def tile(name, shape, dtype, tag=None):
+            return keep.tile(shape, dtype, name=name, tag=tag or name, align_bytes=64)
 
-        w1_raw = tile("w1_raw", [P, PACK, H], F32)
-        nc.sync.dma_start(out=w1_raw[:], in_=w1.rearrange("(p j) c -> p j c", j=PACK))
         offs_sb = tile("offs_sb", [P, S // 16], U16)
         nc.sync.dma_start(offs_sb[:], offs)
         xs_all = tile("xs_all", [P, T], U8)
-        nc.vector.memset(xs_all[:].bitcast(I32), 0)
+        nc.gpsimd.memset(xs_all[:].bitcast(I32), 0)
+        xs_rows = tile("xs_rows", [P, T], U8)
         for q in range(4):
-            nc.scalar.dma_start(
-                out=xs_all[32 * q : 32 * q + 4, :].bitcast(I32),
+            nc.sync.dma_start(
+                out=xs_rows[32 * q : 32 * q + 4, :].bitcast(I32),
                 in_=x_scales[0, 4 * q : 4 * q + 4, :].bitcast(I32),
             )
+        for q in range(4):
+            nc.vector.tensor_copy(
+                out=xs_all[32 * q : 32 * q + 4, :].bitcast(I32),
+                in_=xs_rows[32 * q : 32 * q + 4, :].bitcast(I32),
+            )
+        w1_raw = tile("w1_raw", [P, PACK, H], F32, tag="raw")
+        nc.sync.dma_start(out=w1_raw[:], in_=w1.rearrange("(p j) c -> p j c", j=PACK))
         xw_all = tile("xw_all", [P, T], U32)
         nc.sync.dma_start(
             out=xw_all[:].bitcast(I32),
@@ -58,8 +65,6 @@ def tile_picked_yretnx_msr_p_kernel(
         nc.sync.dma_start(far_sb[:], far)
         unit_sb = tile("unit_sb", [P, PACK], F32)
         nc.sync.dma_start(out=unit_sb[:], in_=unit.rearrange("(p t) o -> p (t o)", t=PACK))
-        w3_raw = tile("w3_raw", [P, PACK, N], F32)
-        nc.sync.dma_start(out=w3_raw[:], in_=w3.rearrange("(p j) n -> p j n", j=PACK))
 
         def copy(on_scalar, dst, src):
             if on_scalar:
@@ -67,13 +72,12 @@ def tile_picked_yretnx_msr_p_kernel(
             else:
                 nc.vector.tensor_copy(out=dst, in_=src)
 
-        def deal(raw, name, engines):
+        def deal(halves, name, engines):
             grouped = tile(name + "_bf", [P, PACK, P, PACK], BF16)
             dst = grouped[:].rearrange("p t m j -> p m j t")
-            src = raw[:].rearrange("p j (m t) -> p m j t", t=PACK)
-            share = P // len(engines)
             for e, on_scalar in enumerate(engines):
-                copy(on_scalar, dst[:, e * share : (e + 1) * share], src[:, e * share : (e + 1) * share])
+                src = halves[e].rearrange("p j (m t) -> p m j t", t=PACK)
+                copy(on_scalar, dst[:, e * P // 2 : (e + 1) * P // 2], src)
             return grouped[:].rearrange("p t m j -> p (t m j)")
 
         def quantize(src, name, width):
@@ -82,33 +86,42 @@ def tile_picked_yretnx_msr_p_kernel(
             nc.vector.quantize_mx(out=codes[:].bitcast(FP8X4), scales=scales[:], in_=src)
             return codes, scales
 
-        w1_codes, w1_scales = quantize(deal(w1_raw, "w1", (False, True)), "w1", H)
+        w1_codes, w1_scales = quantize(deal((w1_raw[:, :, : H // 2], w1_raw[:, :, H // 2 :]), "w1", (False, True)), "w1", H)
+        w3_raw = tile("w3_raw", [P, PACK, N], F32, tag="raw")
+        nc.sync.dma_start(out=w3_raw[:], in_=w3.rearrange("(p j) n -> p j n", j=PACK))
 
         xs = tile("xs", [P, S], U8)
         nc.vector.tensor_copy(xs[:], xs_all[:].indirect(offs_sb[:]))
         xw = tile("xw", [P, S], U32)
-        nc.vector.tensor_copy(xw[:], xw_all[:].indirect(offs_sb[:]))
+        halves = (slice(0, HALF), slice(HALF, S))
+        for e in range(2):
+            nc.vector.tensor_copy(xw[:, halves[e]], xw_all[:].indirect(offs_sb[:, e * HALF // 16 : (e + 1) * HALF // 16]))
 
-        def product(bank, codes, scales, t):
+        def product(bank, codes, scales, t, pix=slice(0, S)):
             cols = slice(t * P, (t + 1) * P)
             nc.tensor.matmul_mx(
-                out=bank[:],
+                out=bank,
                 lhsT=codes[:, cols].bitcast(FP8X4),
                 lhsT_scale=scales[:, cols],
-                rhs=xw[:].bitcast(FP8X4),
-                rhs_scale=xs[:],
+                rhs=xw[:, pix].bitcast(FP8X4),
+                rhs_scale=xs[:, pix],
                 start=True,
                 stop=True,
             )
 
         y = [psum.tile([P, S], F32, name="y%d" % t, tag="bank%d" % t) for t in range(PACK)]
-        for t in range(PACK):
-            product(y[t], w1_codes, w1_scales, t)
+        y_early = psum.tile([P, HALF], F32, name="y_early", tag="bank%d" % (2 * PACK - 1))
+        product(y_early[:], w1_codes, w1_scales, 0, halves[0])
+        product(y[0][:, halves[1]], w1_codes, w1_scales, 0, halves[1])
+        for t in range(1, PACK):
+            product(y[t][:], w1_codes, w1_scales, t)
+        th = [tile("th%d" % t, [P, 2 * S], F32) for t in range(PACK)]
+        nc.scalar.activation(th[0][:, halves[0]], y_early[:], ACT.Tanh)
 
-        w2_codes, w2_scales = quantize(deal(w2_raw, "w2", (False,)), "w2", H)
+        w2_codes, w2_scales = quantize(deal((w2_raw[:, :, : H // 2], w2_raw[:, :, H // 2 :]), "w2", (False, False)), "w2", H)
         ys = [psum.tile([P, S], F32, name="ys%d" % t, tag="bank%d" % (PACK + t)) for t in range(PACK)]
         for t in range(PACK):
-            product(ys[t], w2_codes, w2_scales, t)
+            product(ys[t][:], w2_codes, w2_scales, t)
 
         u8 = tile("u8", [P, PACK], F32)
         u4 = tile("u4", [P, PACK], F32)
@@ -116,7 +129,7 @@ def tile_picked_yretnx_msr_p_kernel(
         for dst, factor in ((u8, 0.8), (u4, 0.4), (u5, 0.5)):
             nc.gpsimd.tensor_scalar(dst[:], unit_sb[:], factor, 0.0, ALU.mult, ALU.add)
 
-        th = [tile("th%d" % t, [P, 2 * S], F32) for t in range(PACK)]
+
         inten = [tile("inten%d" % t, [P, S + SPARE], F32) for t in range(PACK)]
         for t in range(PACK):
             nc.gpsimd.memset(inten[t][:, S:], 0.0)
@@ -129,55 +142,67 @@ def tile_picked_yretnx_msr_p_kernel(
         log_sur = tile("log_sur", [P, PACK, S], F32)
         near_term = tile("near_term", [P, PACK, S], F32)
 
+        def bound(t):
+            pix = halves[1] if t == 0 else slice(0, S)
+            nc.scalar.activation(th[t][:, pix], y[t][:, pix], ACT.Tanh)
+
+        def mixing(t):
+            nc.scalar.activation(th[t][:, S:], ys[t][:], ACT.Tanh, scale=0.5)
+
         def surround(t):
-            nc.scalar.activation(th[t][:, :S], y[t][:], ACT.Tanh)
             nc.scalar.activation(inten[t][:, :S], th[t][:, :S], ACT.Exp, scale=0.8)
             nc.scalar.activation(near[:, t, :], inten[t][:].indirect(s1_sb[:]), ACT.Copy)
             nc.vector.tensor_tensor(both[:, t, :], inten[t][:].indirect(s2_sb[:]), near[:, t, :], ALU.add)
 
-        def mixing(t):
-            nc.scalar.activation(th[t][:, S:], ys[t][:], ACT.Tanh, scale=0.5)
-            nc.vector.tensor_scalar(far_w[:, t, :], th[t][:, S:], -1.0, u4[:, t : t + 1], ALU.add, ALU.mult)
-
         def far_side(t):
+            nc.vector.tensor_scalar(far_w[:, t, :], th[t][:, S:], -1.0, u4[:, t : t + 1], ALU.add, ALU.mult)
             nc.vector.tensor_tensor(far_term[:, t, :], th[t][:].indirect(far_sb[:]), far_w[:, t, :], ALU.mult)
             nc.vector.scalar_tensor_tensor(
                 part[:, t, :], th[t][:, :S], u8[:, t : t + 1], far_term[:, t, :], ALU.mult, ALU.add
             )
 
-        surround(0)
         for t in range(PACK):
+            bound(t)
+            surround(t)
             mixing(t)
-            if t + 1 < PACK:
-                surround(t + 1)
             far_side(t)
 
         w3_bf = tile("w3_bf", [P, N, PACK], BF16)
-        nc.scalar.copy(
+        nc.vector.tensor_copy(
             out=w3_bf[:].rearrange("p (c i) j -> p c j i", i=4),
             in_=w3_raw[:].rearrange("p j (c i) -> p c j i", i=4),
         )
         w3_codes, w3_scales = quantize(w3_bf[:].rearrange("p n j -> p (n j)"), "w3", N)
 
-        for t in range(PACK):
-            nc.scalar.activation(
-                near_w[:, t, :], th[t][:, S:], ACT.Identity, bias=u5[:, t : t + 1], scale=u5[:, t : t + 1]
-            )
+        starts = [sum(CHUNKS[:n]) for n in range(len(CHUNKS))]
+        spans = [slice(c, c + w) for c, w in zip(starts, CHUNKS)]
+        hid = [tile("hid%d" % n, [P, w, PACK], BF16) for n, w in enumerate(CHUNKS)]
 
-        c0 = 0
-        for n, width in enumerate(CHUNKS):
-            cols = slice(c0, c0 + width)
-            c0 += width
+        def near_side(e):
+            cols = halves[e]
             nc.scalar.activation(log_sur[:, :, cols], both[:, :, cols], ACT.Ln, scale=0.5)
+            for t in range(PACK):
+                nc.scalar.activation(
+                    near_w[:, t, cols],
+                    th[t][:, S + cols.start : S + cols.stop],
+                    ACT.Identity,
+                    bias=u5[:, t : t + 1],
+                    scale=u5[:, t : t + 1],
+                )
             nc.vector.tensor_tensor(near_term[:, :, cols], near_w[:, :, cols], log_sur[:, :, cols], ALU.mult)
-            hid = tile("hid%d" % n, [P, width, PACK], BF16)
+
+        def mix(n):
+            cols = spans[n]
             nc.vector.tensor_tensor(
-                hid[:].rearrange("p (c i) t -> p c t i", i=4),
+                hid[n][:].rearrange("p (c i) t -> p c t i", i=4),
                 part[:, :, cols].rearrange("p t (c i) -> p c t i", i=4),
                 near_term[:, :, cols].rearrange("p t (c i) -> p c t i", i=4),
                 ALU.subtract,
             )
-            hid_codes, hid_scales = quantize(hid[:].rearrange("p c t -> p (c t)"), "hid%d" % n, width)
+
+        def finish(n):
+            width = CHUNKS[n]
+            hid_codes, hid_scales = quantize(hid[n][:].rearrange("p c t -> p (c t)"), "hid%d" % n, width)
             acc = psum.tile([P, width], F32, name="acc%d" % n, tag="bank%d" % n)
             nc.tensor.matmul_mx(
                 out=acc[:],
@@ -190,4 +215,13 @@ def tile_picked_yretnx_msr_p_kernel(
             )
             res = tile("res%d" % n, [P, width], F32)
             nc.scalar.copy(out=res[:], in_=acc[:])
-            nc.sync.dma_start(out=out[:, cols], in_=res[:])
+            nc.sync.dma_start(out=out[:, spans[n]], in_=res[:])
+
+        near_side(0)
+        mix(0)
+        near_side(1)
+        finish(0)
+        mix(1)
+        mix(2)
+        finish(1)
+        finish(2)

@@ -17,8 +17,7 @@ ALU = mybir.AluOpType
 
 P = 128
 PACK = 4
-SPARE = 16
-CHUNKS = (256, 128, 128)
+CHUNKS = (128, 256, 128)
 HALF = S // 2
 
 
@@ -50,7 +49,7 @@ def tile_picked_yretnx_msr_p_kernel(
             )
         w1_raw = tile("w1_raw", [P, PACK, H], F32, tag="raw")
         nc.sync.dma_start(out=w1_raw[:], in_=w1.rearrange("(p j) c -> p j c", j=PACK))
-        xw_all = tile("xw_all", [P, T], U32)
+        xw_all = tile("xw_all", [P, T], U32, tag="table")
         nc.sync.dma_start(
             out=xw_all[:].bitcast(I32),
             in_=x_words[0].rearrange("p n t -> p (n t)").bitcast(I32),
@@ -72,8 +71,8 @@ def tile_picked_yretnx_msr_p_kernel(
             else:
                 nc.vector.tensor_copy(out=dst, in_=src)
 
-        def deal(halves, name, engines):
-            grouped = tile(name + "_bf", [P, PACK, P, PACK], BF16)
+        def deal(halves, name, engines, tag):
+            grouped = tile(name + "_bf", [P, PACK, P, PACK], BF16, tag=tag)
             dst = grouped[:].rearrange("p t m j -> p m j t")
             for e, on_scalar in enumerate(engines):
                 src = halves[e].rearrange("p j (m t) -> p m j t", t=PACK)
@@ -86,13 +85,13 @@ def tile_picked_yretnx_msr_p_kernel(
             nc.vector.quantize_mx(out=codes[:].bitcast(FP8X4), scales=scales[:], in_=src)
             return codes, scales
 
-        w1_codes, w1_scales = quantize(deal((w1_raw[:, :, : H // 2], w1_raw[:, :, H // 2 :]), "w1", (False, True)), "w1", H)
+        w1_codes, w1_scales = quantize(deal((w1_raw[:, :, : H // 2], w1_raw[:, :, H // 2 :]), "w1", (False, True), "stage"), "w1", H)
         w3_raw = tile("w3_raw", [P, PACK, N], F32, tag="raw")
         nc.sync.dma_start(out=w3_raw[:], in_=w3.rearrange("(p j) n -> p j n", j=PACK))
 
         xs = tile("xs", [P, S], U8)
         nc.vector.tensor_copy(xs[:], xs_all[:].indirect(offs_sb[:]))
-        xw = tile("xw", [P, S], U32)
+        xw = tile("xw", [P, S], U32, tag="stage")
         halves = (slice(0, HALF), slice(HALF, S))
         for e in range(2):
             nc.vector.tensor_copy(xw[:, halves[e]], xw_all[:].indirect(offs_sb[:, e * HALF // 16 : (e + 1) * HALF // 16]))
@@ -115,10 +114,10 @@ def tile_picked_yretnx_msr_p_kernel(
         product(y[0][:, halves[1]], w1_codes, w1_scales, 0, halves[1])
         for t in range(1, PACK):
             product(y[t][:], w1_codes, w1_scales, t)
-        th = [tile("th%d" % t, [P, 2 * S], F32) for t in range(PACK)]
+        th = [tile("th%d" % t, [P, S], F32) for t in range(PACK)]
         nc.scalar.activation(th[0][:, halves[0]], y_early[:], ACT.Tanh)
 
-        w2_codes, w2_scales = quantize(deal((w2_raw[:, :, : H // 2], w2_raw[:, :, H // 2 :]), "w2", (False, False)), "w2", H)
+        w2_codes, w2_scales = quantize(deal((w2_raw[:, :, : H // 2], w2_raw[:, :, H // 2 :]), "w2", (False, False), "table"), "w2", H)
         ys = [psum.tile([P, S], F32, name="ys%d" % t, tag="bank%d" % (PACK + t)) for t in range(PACK)]
         for t in range(PACK):
             product(ys[t][:], w2_codes, w2_scales, t)
@@ -130,10 +129,14 @@ def tile_picked_yretnx_msr_p_kernel(
             nc.gpsimd.tensor_scalar(dst[:], unit_sb[:], factor, 0.0, ALU.mult, ALU.add)
 
 
-        inten = [tile("inten%d" % t, [P, S + SPARE], F32) for t in range(PACK)]
-        for t in range(PACK):
-            nc.gpsimd.memset(inten[t][:, S:], 0.0)
-        near = tile("near", [P, PACK, S], F32)
+        slope = tile("slope", [P, 1], F32)
+        ones = tile("ones", [P, 1], F32)
+        nc.gpsimd.memset(ones[:], 1.0)
+        nc.gpsimd.tensor_scalar(slope[:], ones[:], 0.8, 0.0, ALU.mult, ALU.add)
+
+        crest = tile("crest", [P, PACK, S], F32)
+        near_a = tile("near_a", [P, PACK, S], F32)
+        near_b = tile("near_b", [P, PACK, S], F32)
         both = tile("both", [P, PACK, S], F32)
         far_w = tile("far_w", [P, PACK, S], F32)
         far_term = tile("far_term", [P, PACK, S], F32)
@@ -142,30 +145,34 @@ def tile_picked_yretnx_msr_p_kernel(
         log_sur = tile("log_sur", [P, PACK, S], F32)
         near_term = tile("near_term", [P, PACK, S], F32)
 
-        def bound(t):
-            pix = halves[1] if t == 0 else slice(0, S)
-            nc.scalar.activation(th[t][:, pix], y[t][:, pix], ACT.Tanh)
-
-        def mixing(t):
-            nc.scalar.activation(th[t][:, S:], ys[t][:], ACT.Tanh, scale=0.5)
+        def entries(offsets, pix):
+            return offsets[:, pix.start // 16 : pix.stop // 16]
 
         def surround(t):
-            nc.scalar.activation(inten[t][:, :S], th[t][:, :S], ACT.Exp, scale=0.8)
-            nc.scalar.activation(near[:, t, :], inten[t][:].indirect(s1_sb[:]), ACT.Copy)
-            nc.vector.tensor_tensor(both[:, t, :], inten[t][:].indirect(s2_sb[:]), near[:, t, :], ALU.add)
+            for dst, offsets in ((near_a, s1_sb), (near_b, s2_sb)):
+                for pix in halves:
+                    nc.scalar.activation(
+                        dst[:, t, pix], th[t][:].indirect(entries(offsets, pix)), ACT.Exp, scale=slope[:]
+                    )
+            nc.vector.tensor_tensor(both[:, t, :], near_a[:, t, :], near_b[:, t, :], ALU.add)
 
         def far_side(t):
-            nc.vector.tensor_scalar(far_w[:, t, :], th[t][:, S:], -1.0, u4[:, t : t + 1], ALU.add, ALU.mult)
-            nc.vector.tensor_tensor(far_term[:, t, :], th[t][:].indirect(far_sb[:]), far_w[:, t, :], ALU.mult)
+            nc.scalar.activation(crest[:, t, :], ys[t][:], ACT.Tanh, scale=0.5)
+            nc.vector.tensor_scalar(far_w[:, t, :], crest[:, t, :], -1.0, u4[:, t : t + 1], ALU.add, ALU.mult)
+            nc.vector.tensor_scalar(near_w[:, t, :], crest[:, t, :], 1.0, u5[:, t : t + 1], ALU.add, ALU.mult)
+            for pix in halves:
+                nc.vector.tensor_tensor(
+                    far_term[:, t, pix], th[t][:].indirect(entries(far_sb, pix)), far_w[:, t, pix], ALU.mult
+                )
             nc.vector.scalar_tensor_tensor(
-                part[:, t, :], th[t][:, :S], u8[:, t : t + 1], far_term[:, t, :], ALU.mult, ALU.add
+                part[:, t, :], th[t][:], u8[:, t : t + 1], far_term[:, t, :], ALU.mult, ALU.add
             )
 
         for t in range(PACK):
-            bound(t)
-            surround(t)
-            mixing(t)
-            far_side(t)
+            pix = halves[1] if t == 0 else slice(0, S)
+            nc.scalar.activation(th[t][:, pix], y[t][:, pix], ACT.Tanh)
+            for stage in (surround, far_side) if t == 0 else (far_side, surround):
+                stage(t)
 
         w3_bf = tile("w3_bf", [P, N, PACK], BF16)
         nc.vector.tensor_copy(
@@ -178,17 +185,9 @@ def tile_picked_yretnx_msr_p_kernel(
         spans = [slice(c, c + w) for c, w in zip(starts, CHUNKS)]
         hid = [tile("hid%d" % n, [P, w, PACK], BF16) for n, w in enumerate(CHUNKS)]
 
-        def near_side(e):
-            cols = halves[e]
+        def near_side(n):
+            cols = spans[n]
             nc.scalar.activation(log_sur[:, :, cols], both[:, :, cols], ACT.Ln, scale=0.5)
-            for t in range(PACK):
-                nc.scalar.activation(
-                    near_w[:, t, cols],
-                    th[t][:, S + cols.start : S + cols.stop],
-                    ACT.Identity,
-                    bias=u5[:, t : t + 1],
-                    scale=u5[:, t : t + 1],
-                )
             nc.vector.tensor_tensor(near_term[:, :, cols], near_w[:, :, cols], log_sur[:, :, cols], ALU.mult)
 
         def mix(n):
@@ -218,10 +217,8 @@ def tile_picked_yretnx_msr_p_kernel(
             nc.sync.dma_start(out=out[:, spans[n]], in_=res[:])
 
         near_side(0)
-        mix(0)
-        near_side(1)
-        finish(0)
-        mix(1)
-        mix(2)
-        finish(1)
-        finish(2)
+        for n in range(len(CHUNKS)):
+            mix(n)
+            if n + 1 < len(CHUNKS):
+                near_side(n + 1)
+            finish(n)

@@ -3,7 +3,7 @@ from contextlib import ExitStack
 import concourse.mybir as mybir
 
 K, T, S, N, H = 512, 2048, 512, 128, 512
-FLOPS = 2 * K * H * S * 2 + 2 * H * N * S
+FLOPS = 2 * (2 * K * H * S) + 2 * H * N * S
 
 F32 = mybir.dt.float32
 BF16 = mybir.dt.bfloat16
@@ -17,8 +17,12 @@ ALU = mybir.AluOpType
 
 P = 128
 PACK = 4
-CHUNKS = (128, 256, 128)
-HALF = S // 2
+LANES = 16
+SPARE = 16
+SHARED = 2
+PIXEL_HALVES = (slice(0, S // 2), slice(S // 2, S))
+LOG_SPANS = (slice(0, 128), slice(128, 256), slice(256, S))
+OUT_SPANS = (slice(0, 256), slice(256, 384), slice(384, S))
 
 
 def tile_picked_yretnx_msr_p_kernel(
@@ -32,193 +36,187 @@ def tile_picked_yretnx_msr_p_kernel(
         def tile(name, shape, dtype, tag=None):
             return keep.tile(shape, dtype, name=name, tag=tag or name, align_bytes=64)
 
-        offs_sb = tile("offs_sb", [P, S // 16], U16)
-        nc.sync.dma_start(offs_sb[:], offs)
-        xs_all = tile("xs_all", [P, T], U8)
-        nc.gpsimd.memset(xs_all[:].bitcast(I32), 0)
-        xs_rows = tile("xs_rows", [P, T], U8)
-        for q in range(4):
-            nc.sync.dma_start(
-                out=xs_rows[32 * q : 32 * q + 4, :].bitcast(I32),
-                in_=x_scales[0, 4 * q : 4 * q + 4, :].bitcast(I32),
+        def bank(name, width, index):
+            return psum.tile([P, width], F32, name=name, tag="bank%d" % index)
+
+        def load_list(name, source):
+            entries = tile(name, [P, S // LANES], U16)
+            nc.sync.dma_start(entries[:], source)
+            return entries
+
+        def load_rows(name, source, tag=None):
+            raw = tile(name, [P, PACK, source.shape[1]], F32, tag)
+            nc.sync.dma_start(out=raw[:], in_=source.rearrange("(p j) c -> p j c", j=PACK))
+            return raw
+
+        def quantize(name, values):
+            width = values.shape[1] // PACK
+            codes = tile(name + "_codes", [P, width], U32)
+            scales = tile(name + "_scales", [P, width], U8)
+            nc.vector.quantize_mx(out=codes[:].bitcast(FP8X4), scales=scales[:], in_=values)
+            return codes, scales
+
+        def multiply(result, stationary, columns, moving, pixels):
+            nc.tensor.matmul_mx(
+                out=result,
+                lhsT=stationary[0][:, columns].bitcast(FP8X4),
+                lhsT_scale=stationary[1][:, columns],
+                rhs=moving[0][:, pixels].bitcast(FP8X4),
+                rhs_scale=moving[1][:, pixels],
+                start=True,
+                stop=True,
             )
-        for q in range(4):
-            nc.vector.tensor_copy(
-                out=xs_all[32 * q : 32 * q + 4, :].bitcast(I32),
-                in_=xs_rows[32 * q : 32 * q + 4, :].bitcast(I32),
-            )
-        w1_raw = tile("w1_raw", [P, PACK, H], F32, tag="raw")
-        nc.sync.dma_start(out=w1_raw[:], in_=w1.rearrange("(p j) c -> p j c", j=PACK))
-        xw_all = tile("xw_all", [P, T], U32, tag="table")
-        nc.sync.dma_start(
-            out=xw_all[:].bitcast(I32),
-            in_=x_words[0].rearrange("p n t -> p (n t)").bitcast(I32),
-        )
-        w2_raw = tile("w2_raw", [P, PACK, H], F32)
-        nc.sync.dma_start(out=w2_raw[:], in_=w2.rearrange("(p j) c -> p j c", j=PACK))
-        s1_sb = tile("s1_sb", [P, S // 16], U16)
-        nc.sync.dma_start(s1_sb[:], s1)
-        s2_sb = tile("s2_sb", [P, S // 16], U16)
-        nc.sync.dma_start(s2_sb[:], s2)
-        far_sb = tile("far_sb", [P, S // 16], U16)
-        nc.sync.dma_start(far_sb[:], far)
+
+        def deal(name, halves, copies, tag):
+            dealt = tile(name, [P, PACK, P, PACK], BF16, tag)
+            walk = dealt[:].rearrange("p t m j -> p m j t")
+            for e in range(2):
+                copies[e](
+                    out=walk[:, e * P // 2 : (e + 1) * P // 2],
+                    in_=halves[e].rearrange("p j (m t) -> p m j t", t=PACK),
+                )
+            return dealt
+
+        offs_sb = load_list("offs_sb", offs)
         unit_sb = tile("unit_sb", [P, PACK], F32)
         nc.sync.dma_start(out=unit_sb[:], in_=unit.rearrange("(p t) o -> p (t o)", t=PACK))
 
-        def copy(on_scalar, dst, src):
-            if on_scalar:
-                nc.scalar.copy(out=dst, in_=src)
-            else:
-                nc.vector.tensor_copy(out=dst, in_=src)
+        scale_table = tile("scale_table", [P, T], U8)
+        nc.gpsimd.memset(scale_table[:].bitcast(I32), 0)
+        scale_rows = tile("scale_rows", [P, T], U8)
+        quadrants = [slice(32 * q, 32 * q + 4) for q in range(4)]
+        for q, rows in enumerate(quadrants):
+            nc.sync.dma_start(out=scale_rows[rows, :].bitcast(I32), in_=x_scales[0, 4 * q : 4 * q + 4, :].bitcast(I32))
+        for rows in quadrants:
+            nc.vector.tensor_copy(out=scale_table[rows, :].bitcast(I32), in_=scale_rows[rows, :].bitcast(I32))
 
-        def deal(halves, name, engines, tag):
-            grouped = tile(name + "_bf", [P, PACK, P, PACK], BF16, tag=tag)
-            dst = grouped[:].rearrange("p t m j -> p m j t")
-            for e, on_scalar in enumerate(engines):
-                src = halves[e].rearrange("p j (m t) -> p m j t", t=PACK)
-                copy(on_scalar, dst[:, e * P // 2 : (e + 1) * P // 2], src)
-            return grouped[:].rearrange("p t m j -> p (t m j)")
+        w2_raw = load_rows("w2_raw", w2, tag="raw")
+        word_table = tile("word_table", [P, T], U32, tag="table")
+        nc.sync.dma_start(
+            out=word_table[:].bitcast(I32), in_=x_words[0].rearrange("p n t -> p (n t)").bitcast(I32)
+        )
+        w1_raw = [load_rows("w1_raw%d" % e, w1[:, e * H // 2 : (e + 1) * H // 2]) for e in range(2)]
+        s1_sb = load_list("s1_sb", s1)
+        s2_sb = load_list("s2_sb", s2)
+        far_sb = load_list("far_sb", far)
 
-        def quantize(src, name, width):
-            codes = tile(name + "_codes", [P, width], U32)
-            scales = tile(name + "_scales", [P, width], U8)
-            nc.vector.quantize_mx(out=codes[:].bitcast(FP8X4), scales=scales[:], in_=src)
-            return codes, scales
-
-        w1_codes, w1_scales = quantize(deal((w1_raw[:, :, : H // 2], w1_raw[:, :, H // 2 :]), "w1", (False, True), "stage"), "w1", H)
-        w3_raw = tile("w3_raw", [P, PACK, N], F32, tag="raw")
-        nc.sync.dma_start(out=w3_raw[:], in_=w3.rearrange("(p j) n -> p j n", j=PACK))
-
-        xs = tile("xs", [P, S], U8)
-        nc.vector.tensor_copy(xs[:], xs_all[:].indirect(offs_sb[:]))
-        xw = tile("xw", [P, S], U32, tag="stage")
-        halves = (slice(0, HALF), slice(HALF, S))
-        for e in range(2):
-            nc.vector.tensor_copy(xw[:, halves[e]], xw_all[:].indirect(offs_sb[:, e * HALF // 16 : (e + 1) * HALF // 16]))
-
-        def product(bank, codes, scales, t, pix=slice(0, S)):
-            cols = slice(t * P, (t + 1) * P)
-            nc.tensor.matmul_mx(
-                out=bank,
-                lhsT=codes[:, cols].bitcast(FP8X4),
-                lhsT_scale=scales[:, cols],
-                rhs=xw[:, pix].bitcast(FP8X4),
-                rhs_scale=xs[:, pix],
-                start=True,
-                stop=True,
-            )
-
-        y = [psum.tile([P, S], F32, name="y%d" % t, tag="bank%d" % t) for t in range(PACK)]
-        y_early = psum.tile([P, HALF], F32, name="y_early", tag="bank%d" % (2 * PACK - 1))
-        product(y_early[:], w1_codes, w1_scales, 0, halves[0])
-        product(y[0][:, halves[1]], w1_codes, w1_scales, 0, halves[1])
-        for t in range(1, PACK):
-            product(y[t][:], w1_codes, w1_scales, t)
-        th = [tile("th%d" % t, [P, S], F32) for t in range(PACK)]
-        nc.scalar.activation(th[0][:, halves[0]], y_early[:], ACT.Tanh)
-
-        w2_codes, w2_scales = quantize(deal((w2_raw[:, :, : H // 2], w2_raw[:, :, H // 2 :]), "w2", (False, False), "table"), "w2", H)
-        ys = [psum.tile([P, S], F32, name="ys%d" % t, tag="bank%d" % (PACK + t)) for t in range(PACK)]
-        for t in range(PACK):
-            product(ys[t][:], w2_codes, w2_scales, t)
-
-        u8 = tile("u8", [P, PACK], F32)
-        u4 = tile("u4", [P, PACK], F32)
-        u5 = tile("u5", [P, PACK], F32)
-        for dst, factor in ((u8, 0.8), (u4, 0.4), (u5, 0.5)):
-            nc.gpsimd.tensor_scalar(dst[:], unit_sb[:], factor, 0.0, ALU.mult, ALU.add)
-
-
-        slope = tile("slope", [P, 1], F32)
+        unit_08, unit_04, unit_05 = [tile("unit_%d" % n, [P, PACK], F32) for n in range(3)]
+        for scaled, factor in ((unit_08, 0.8), (unit_04, 0.4), (unit_05, 0.5)):
+            nc.scalar.activation(scaled[:], unit_sb[:], ACT.Copy, scale=factor)
         ones = tile("ones", [P, 1], F32)
+        slope = tile("slope", [P, 1], F32)
         nc.gpsimd.memset(ones[:], 1.0)
         nc.gpsimd.tensor_scalar(slope[:], ones[:], 0.8, 0.0, ALU.mult, ALU.add)
+        inten = [tile("inten%d" % t, [P, S + SPARE], F32) for t in range(SHARED)]
+        for t in range(SHARED):
+            nc.gpsimd.memset(inten[t][:, S:], 0.0)
 
-        crest = tile("crest", [P, PACK, S], F32)
+        w2_dealt = deal(
+            "w2_dealt",
+            (w2_raw[:, :, : H // 2], w2_raw[:, :, H // 2 :]),
+            (nc.vector.tensor_copy, nc.scalar.copy),
+            tag="stage",
+        )
+        w2_mx = quantize("w2", w2_dealt[:].rearrange("p t m j -> p (t m j)"))
+        w3_raw = load_rows("w3_raw", w3, tag="raw")
+
+        x_bytes = tile("x_bytes", [P, S], U8)
+        nc.vector.tensor_copy(x_bytes[:], scale_table[:].indirect(offs_sb[:]))
+        x_codes = tile("x_codes", [P, S], U32, tag="stage")
+        for pixels in PIXEL_HALVES:
+            entries = offs_sb[:, pixels.start // LANES : pixels.stop // LANES]
+            nc.vector.tensor_copy(x_codes[:, pixels], word_table[:].indirect(entries))
+        x_mx = (x_codes, x_bytes)
+
+        pair = [tile("pair%d" % t, [P, 2 * S], F32) for t in range(PACK)]
+        bound = [pair[t][:, :S] for t in range(PACK)]
+        swing = [pair[t][:, S:] for t in range(PACK)]
+        features = [slice(t * P, (t + 1) * P) for t in range(PACK)]
+
+        ys_first = bank("ys_first", S // 2, 2 * PACK - 1)
+        ys = [bank("ys%d" % t, S, t) for t in range(PACK)]
+        pieces = [(0, PIXEL_HALVES[0], ys_first[:]), (0, PIXEL_HALVES[1], ys[0][:, PIXEL_HALVES[1]])]
+        pieces.extend((t, slice(0, S), ys[t][:]) for t in range(1, PACK))
+        for t, pixels, result in pieces:
+            multiply(result, w2_mx, features[t], x_mx, pixels)
+        for t, pixels, result in pieces:
+            nc.scalar.activation(swing[t][:, pixels], result, ACT.Tanh, scale=0.5)
+
+        w1_dealt = deal(
+            "w1_dealt", (w1_raw[0][:], w1_raw[1][:]), (nc.vector.tensor_copy, nc.vector.tensor_copy), tag="table"
+        )
+        y = [bank("y%d" % t, S, PACK + t) for t in range(PACK)]
+        for e in range(2):
+            w1_mx = quantize("w1_%d" % e, w1_dealt[:, 2 * e : 2 * e + 2].rearrange("p t m j -> p (t m j)"))
+            for t in range(2):
+                multiply(y[2 * e + t][:], w1_mx, features[t], x_mx, slice(0, S))
+
+        weights = tile("weights", [P, 2, PACK, S], F32, tag="table")
+        far_weight, near_weight = weights[:, 0], weights[:, 1]
+        for t in range(PACK):
+            nc.vector.tensor_scalar(far_weight[:, t, :], swing[t], -1.0, unit_04[:, t : t + 1], ALU.add, ALU.mult)
+            nc.vector.tensor_scalar(near_weight[:, t, :], swing[t], 1.0, unit_05[:, t : t + 1], ALU.add, ALU.mult)
+
         near_a = tile("near_a", [P, PACK, S], F32)
-        near_b = tile("near_b", [P, PACK, S], F32)
-        both = tile("both", [P, PACK, S], F32)
-        far_w = tile("far_w", [P, PACK, S], F32)
-        far_term = tile("far_term", [P, PACK, S], F32)
-        part = tile("part", [P, PACK, S], F32)
-        near_w = tile("near_w", [P, PACK, S], F32)
-        log_sur = tile("log_sur", [P, PACK, S], F32)
-        near_term = tile("near_term", [P, PACK, S], F32)
-
-        def entries(offsets, pix):
-            return offsets[:, pix.start // 16 : pix.stop // 16]
-
-        def surround(t):
-            for dst, offsets in ((near_a, s1_sb), (near_b, s2_sb)):
-                for pix in halves:
-                    nc.scalar.activation(
-                        dst[:, t, pix], th[t][:].indirect(entries(offsets, pix)), ACT.Exp, scale=slope[:]
-                    )
-            nc.vector.tensor_tensor(both[:, t, :], near_a[:, t, :], near_b[:, t, :], ALU.add)
-
-        def far_side(t):
-            nc.scalar.activation(crest[:, t, :], ys[t][:], ACT.Tanh, scale=0.5)
-            nc.vector.tensor_scalar(far_w[:, t, :], crest[:, t, :], -1.0, u4[:, t : t + 1], ALU.add, ALU.mult)
-            nc.vector.tensor_scalar(near_w[:, t, :], crest[:, t, :], 1.0, u5[:, t : t + 1], ALU.add, ALU.mult)
-            for pix in halves:
-                nc.vector.tensor_tensor(
-                    far_term[:, t, pix], th[t][:].indirect(entries(far_sb, pix)), far_w[:, t, pix], ALU.mult
-                )
+        near_b = tile("near_b", [P, PACK - SHARED, S], F32, tag="late")
+        near_sum = tile("near_sum", [P, PACK, S], F32)
+        far_tile = tile("far_tile", [P, PACK - 1, S], F32)
+        far_term = [far_tile[:, t, :] for t in range(PACK - 1)] + [near_a[:, PACK - 1, :]]
+        own_and_far = tile("own_and_far", [P, PACK, S], F32)
+        for t in range(PACK):
+            nc.scalar.activation(bound[t], y[t][:], ACT.Tanh)
+            if t < SHARED:
+                nc.scalar.activation(inten[t][:, :S], bound[t], ACT.Exp, scale=0.8)
+                nc.scalar.activation(near_a[:, t, :], inten[t][:].indirect(s1_sb[:]), ACT.Copy)
+                nc.vector.tensor_tensor(near_sum[:, t, :], inten[t][:].indirect(s2_sb[:]), near_a[:, t, :], ALU.add)
+            else:
+                other = near_b[:, t - SHARED, :]
+                nc.scalar.activation(near_a[:, t, :], pair[t][:].indirect(s1_sb[:]), ACT.Exp, scale=slope[:])
+                nc.scalar.activation(other, pair[t][:].indirect(s2_sb[:]), ACT.Exp, scale=slope[:])
+                nc.vector.tensor_tensor(near_sum[:, t, :], near_a[:, t, :], other, ALU.add)
+            nc.vector.tensor_tensor(far_term[t], pair[t][:].indirect(far_sb[:]), far_weight[:, t, :], ALU.mult)
             nc.vector.scalar_tensor_tensor(
-                part[:, t, :], th[t][:], u8[:, t : t + 1], far_term[:, t, :], ALU.mult, ALU.add
+                own_and_far[:, t, :], bound[t], unit_08[:, t : t + 1], far_term[t], ALU.mult, ALU.add
             )
 
-        for t in range(PACK):
-            pix = halves[1] if t == 0 else slice(0, S)
-            nc.scalar.activation(th[t][:, pix], y[t][:, pix], ACT.Tanh)
-            for stage in (surround, far_side) if t == 0 else (far_side, surround):
-                stage(t)
+        log_sur = tile("log_sur", [P, PACK, S], F32)
+        near_term = tile("near_term", [P, PACK, S], F32)
+        hid = [tile("hid%d" % n, [P, span.stop - span.start, PACK], BF16) for n, span in enumerate(OUT_SPANS)]
 
-        w3_bf = tile("w3_bf", [P, N, PACK], BF16)
-        nc.vector.tensor_copy(
-            out=w3_bf[:].rearrange("p (c i) j -> p c j i", i=4),
-            in_=w3_raw[:].rearrange("p j (c i) -> p c j i", i=4),
-        )
-        w3_codes, w3_scales = quantize(w3_bf[:].rearrange("p n j -> p (n j)"), "w3", N)
-
-        starts = [sum(CHUNKS[:n]) for n in range(len(CHUNKS))]
-        spans = [slice(c, c + w) for c, w in zip(starts, CHUNKS)]
-        hid = [tile("hid%d" % n, [P, w, PACK], BF16) for n, w in enumerate(CHUNKS)]
-
-        def near_side(n):
-            cols = spans[n]
-            nc.scalar.activation(log_sur[:, :, cols], both[:, :, cols], ACT.Ln, scale=0.5)
-            nc.vector.tensor_tensor(near_term[:, :, cols], near_w[:, :, cols], log_sur[:, :, cols], ALU.mult)
+        def near_side(pixels):
+            nc.scalar.activation(log_sur[:, :, pixels], near_sum[:, :, pixels], ACT.Ln, scale=0.5)
+            nc.vector.tensor_tensor(near_term[:, :, pixels], near_weight[:, :, pixels], log_sur[:, :, pixels], ALU.mult)
 
         def mix(n):
-            cols = spans[n]
+            pixels = OUT_SPANS[n]
             nc.vector.tensor_tensor(
                 hid[n][:].rearrange("p (c i) t -> p c t i", i=4),
-                part[:, :, cols].rearrange("p t (c i) -> p c t i", i=4),
-                near_term[:, :, cols].rearrange("p t (c i) -> p c t i", i=4),
+                own_and_far[:, :, pixels].rearrange("p t (c i) -> p c t i", i=4),
+                near_term[:, :, pixels].rearrange("p t (c i) -> p c t i", i=4),
                 ALU.subtract,
             )
 
-        def finish(n):
-            width = CHUNKS[n]
-            hid_codes, hid_scales = quantize(hid[n][:].rearrange("p c t -> p (c t)"), "hid%d" % n, width)
-            acc = psum.tile([P, width], F32, name="acc%d" % n, tag="bank%d" % n)
-            nc.tensor.matmul_mx(
-                out=acc[:],
-                lhsT=w3_codes[:].bitcast(FP8X4),
-                lhsT_scale=w3_scales[:],
-                rhs=hid_codes[:].bitcast(FP8X4),
-                rhs_scale=hid_scales[:],
-                start=True,
-                stop=True,
-            )
-            res = tile("res%d" % n, [P, width], F32)
-            nc.scalar.copy(out=res[:], in_=acc[:])
-            nc.sync.dma_start(out=out[:, spans[n]], in_=res[:])
+        def finish(n, w3_mx):
+            width = OUT_SPANS[n].stop - OUT_SPANS[n].start
+            hid_mx = quantize("hid%d" % n, hid[n][:].rearrange("p c t -> p (c t)"))
+            channels = bank("channels%d" % n, width, n)
+            multiply(channels[:], w3_mx, slice(0, N), hid_mx, slice(0, width))
+            result = tile("result%d" % n, [P, width], F32)
+            nc.scalar.copy(out=result[:], in_=channels[:])
+            nc.sync.dma_start(out=out[:, OUT_SPANS[n]], in_=result[:])
 
-        near_side(0)
-        for n in range(len(CHUNKS)):
-            mix(n)
-            if n + 1 < len(CHUNKS):
-                near_side(n + 1)
-            finish(n)
+        near_side(LOG_SPANS[0])
+        near_side(LOG_SPANS[1])
+        mix(0)
+        near_side(LOG_SPANS[2])
+        w3_dealt = tile("w3_dealt", [P, N, PACK], BF16, tag="late")
+        nc.scalar.copy(
+            out=w3_dealt[:].rearrange("p (c i) j -> p c j i", i=4),
+            in_=w3_raw[:].rearrange("p j (c i) -> p c j i", i=4),
+        )
+        w3_mx = quantize("w3", w3_dealt[:].rearrange("p n j -> p (n j)"))
+        finish(0, w3_mx)
+        mix(1)
+        mix(2)
+        finish(1, w3_mx)
+        finish(2, w3_mx)

from contextlib import ExitStack

import concourse.mybir as mybir

K, T, S, N, H = 512, 2048, 512, 128, 512
FLOPS = 2 * (2 * K * H * S) + 2 * H * N * S

F32 = mybir.dt.float32
BF16 = mybir.dt.bfloat16
I32 = mybir.dt.int32
U32 = mybir.dt.uint32
U16 = mybir.dt.uint16
U8 = mybir.dt.uint8
FP8X4 = mybir.dt.float8_e4m3fn_x4
ACT = mybir.ActivationFunctionType
ALU = mybir.AluOpType

P = 128
PACK = 4
LANES = 16
SPARE = 16
SHARED = 2
PIXEL_HALVES = (slice(0, S // 2), slice(S // 2, S))
LOG_SPANS = (slice(0, 128), slice(128, 256), slice(256, S))
OUT_SPANS = (slice(0, 256), slice(256, 384), slice(384, S))


def tile_picked_yretnx_msr_p_kernel(
    tc, x_words, x_scales, w1, w2, unit, w3, offs, s1, s2, far, out
):
    nc = tc.nc
    with ExitStack() as ctx:
        keep = ctx.enter_context(tc.tile_pool(name="keep", bufs=1))
        psum = ctx.enter_context(tc.psum_pool(name="psum", bufs=1))

        def tile(name, shape, dtype, tag=None):
            return keep.tile(shape, dtype, name=name, tag=tag or name, align_bytes=64)

        def bank(name, width, index):
            return psum.tile([P, width], F32, name=name, tag="bank%d" % index)

        def load_list(name, source):
            entries = tile(name, [P, S // LANES], U16)
            nc.sync.dma_start(entries[:], source)
            return entries

        def load_rows(name, source, tag=None):
            raw = tile(name, [P, PACK, source.shape[1]], F32, tag)
            nc.sync.dma_start(out=raw[:], in_=source.rearrange("(p j) c -> p j c", j=PACK))
            return raw

        def quantize(name, values):
            width = values.shape[1] // PACK
            codes = tile(name + "_codes", [P, width], U32)
            scales = tile(name + "_scales", [P, width], U8)
            nc.vector.quantize_mx(out=codes[:].bitcast(FP8X4), scales=scales[:], in_=values)
            return codes, scales

        def multiply(result, stationary, columns, moving, pixels):
            nc.tensor.matmul_mx(
                out=result,
                lhsT=stationary[0][:, columns].bitcast(FP8X4),
                lhsT_scale=stationary[1][:, columns],
                rhs=moving[0][:, pixels].bitcast(FP8X4),
                rhs_scale=moving[1][:, pixels],
                start=True,
                stop=True,
            )

        def deal(name, halves, copies, tag):
            dealt = tile(name, [P, PACK, P, PACK], BF16, tag)
            walk = dealt[:].rearrange("p t m j -> p m j t")
            for e in range(2):
                copies[e](
                    out=walk[:, e * P // 2 : (e + 1) * P // 2],
                    in_=halves[e].rearrange("p j (m t) -> p m j t", t=PACK),
                )
            return dealt

        offs_sb = load_list("offs_sb", offs)
        unit_sb = tile("unit_sb", [P, PACK], F32)
        nc.sync.dma_start(out=unit_sb[:], in_=unit.rearrange("(p t) o -> p (t o)", t=PACK))

        scale_table = tile("scale_table", [P, T], U8)
        nc.gpsimd.memset(scale_table[:].bitcast(I32), 0)
        scale_rows = tile("scale_rows", [P, T], U8)
        quadrants = [slice(32 * q, 32 * q + 4) for q in range(4)]
        for q, rows in enumerate(quadrants):
            nc.sync.dma_start(out=scale_rows[rows, :].bitcast(I32), in_=x_scales[0, 4 * q : 4 * q + 4, :].bitcast(I32))
        for rows in quadrants:
            nc.vector.tensor_copy(out=scale_table[rows, :].bitcast(I32), in_=scale_rows[rows, :].bitcast(I32))

        w2_raw = load_rows("w2_raw", w2, tag="raw")
        word_table = tile("word_table", [P, T], U32, tag="table")
        nc.sync.dma_start(
            out=word_table[:].bitcast(I32), in_=x_words[0].rearrange("p n t -> p (n t)").bitcast(I32)
        )
        w1_raw = [load_rows("w1_raw%d" % e, w1[:, e * H // 2 : (e + 1) * H // 2]) for e in range(2)]
        s1_sb = load_list("s1_sb", s1)
        s2_sb = load_list("s2_sb", s2)
        far_sb = load_list("far_sb", far)

        unit_08, unit_04, unit_05 = [tile("unit_%d" % n, [P, PACK], F32) for n in range(3)]
        for scaled, factor in ((unit_08, 0.8), (unit_04, 0.4), (unit_05, 0.5)):
            nc.scalar.activation(scaled[:], unit_sb[:], ACT.Copy, scale=factor)
        ones = tile("ones", [P, 1], F32)
        slope = tile("slope", [P, 1], F32)
        nc.gpsimd.memset(ones[:], 1.0)
        nc.gpsimd.tensor_scalar(slope[:], ones[:], 0.8, 0.0, ALU.mult, ALU.add)
        inten = [tile("inten%d" % t, [P, S + SPARE], F32) for t in range(SHARED)]
        for t in range(SHARED):
            nc.gpsimd.memset(inten[t][:, S:], 0.0)

        w2_dealt = deal(
            "w2_dealt",
            (w2_raw[:, :, : H // 2], w2_raw[:, :, H // 2 :]),
            (nc.vector.tensor_copy, nc.scalar.copy),
            tag="stage",
        )
        w2_mx = quantize("w2", w2_dealt[:].rearrange("p t m j -> p (t m j)"))
        w3_raw = load_rows("w3_raw", w3, tag="raw")

        x_bytes = tile("x_bytes", [P, S], U8)
        nc.vector.tensor_copy(x_bytes[:], scale_table[:].indirect(offs_sb[:]))
        x_codes = tile("x_codes", [P, S], U32, tag="stage")
        for pixels in PIXEL_HALVES:
            entries = offs_sb[:, pixels.start // LANES : pixels.stop // LANES]
            nc.vector.tensor_copy(x_codes[:, pixels], word_table[:].indirect(entries))
        x_mx = (x_codes, x_bytes)

        pair = [tile("pair%d" % t, [P, 2 * S], F32) for t in range(PACK)]
        bound = [pair[t][:, :S] for t in range(PACK)]
        swing = [pair[t][:, S:] for t in range(PACK)]
        features = [slice(t * P, (t + 1) * P) for t in range(PACK)]

        ys_first = bank("ys_first", S // 2, 2 * PACK - 1)
        ys = [bank("ys%d" % t, S, t) for t in range(PACK)]
        pieces = [(0, PIXEL_HALVES[0], ys_first[:]), (0, PIXEL_HALVES[1], ys[0][:, PIXEL_HALVES[1]])]
        pieces.extend((t, slice(0, S), ys[t][:]) for t in range(1, PACK))
        for t, pixels, result in pieces:
            multiply(result, w2_mx, features[t], x_mx, pixels)
        for t, pixels, result in pieces:
            nc.scalar.activation(swing[t][:, pixels], result, ACT.Tanh, scale=0.5)

        w1_dealt = deal(
            "w1_dealt", (w1_raw[0][:], w1_raw[1][:]), (nc.vector.tensor_copy, nc.vector.tensor_copy), tag="table"
        )
        y = [bank("y%d" % t, S, PACK + t) for t in range(PACK)]
        for e in range(2):
            w1_mx = quantize("w1_%d" % e, w1_dealt[:, 2 * e : 2 * e + 2].rearrange("p t m j -> p (t m j)"))
            for t in range(2):
                multiply(y[2 * e + t][:], w1_mx, features[t], x_mx, slice(0, S))

        weights = tile("weights", [P, 2, PACK, S], F32, tag="table")
        far_weight, near_weight = weights[:, 0], weights[:, 1]
        for t in range(PACK):
            nc.vector.tensor_scalar(far_weight[:, t, :], swing[t], -1.0, unit_04[:, t : t + 1], ALU.add, ALU.mult)
            nc.vector.tensor_scalar(near_weight[:, t, :], swing[t], 1.0, unit_05[:, t : t + 1], ALU.add, ALU.mult)

        near_a = tile("near_a", [P, PACK, S], F32)
        near_b = tile("near_b", [P, PACK - SHARED, S], F32, tag="late")
        near_sum = tile("near_sum", [P, PACK, S], F32)
        far_tile = tile("far_tile", [P, PACK - 1, S], F32)
        far_term = [far_tile[:, t, :] for t in range(PACK - 1)] + [near_a[:, PACK - 1, :]]
        own_and_far = tile("own_and_far", [P, PACK, S], F32)
        for t in range(PACK):
            nc.scalar.activation(bound[t], y[t][:], ACT.Tanh)
            if t < SHARED:
                nc.scalar.activation(inten[t][:, :S], bound[t], ACT.Exp, scale=0.8)
                nc.scalar.activation(near_a[:, t, :], inten[t][:].indirect(s1_sb[:]), ACT.Copy)
                nc.vector.tensor_tensor(near_sum[:, t, :], inten[t][:].indirect(s2_sb[:]), near_a[:, t, :], ALU.add)
            else:
                other = near_b[:, t - SHARED, :]
                nc.scalar.activation(near_a[:, t, :], pair[t][:].indirect(s1_sb[:]), ACT.Exp, scale=slope[:])
                nc.scalar.activation(other, pair[t][:].indirect(s2_sb[:]), ACT.Exp, scale=slope[:])
                nc.vector.tensor_tensor(near_sum[:, t, :], near_a[:, t, :], other, ALU.add)
            nc.vector.tensor_tensor(far_term[t], pair[t][:].indirect(far_sb[:]), far_weight[:, t, :], ALU.mult)
            nc.vector.scalar_tensor_tensor(
                own_and_far[:, t, :], bound[t], unit_08[:, t : t + 1], far_term[t], ALU.mult, ALU.add
            )

        log_sur = tile("log_sur", [P, PACK, S], F32)
        near_term = tile("near_term", [P, PACK, S], F32)
        hid = [tile("hid%d" % n, [P, span.stop - span.start, PACK], BF16) for n, span in enumerate(OUT_SPANS)]

        def near_side(pixels):
            nc.scalar.activation(log_sur[:, :, pixels], near_sum[:, :, pixels], ACT.Ln, scale=0.5)
            nc.vector.tensor_tensor(near_term[:, :, pixels], near_weight[:, :, pixels], log_sur[:, :, pixels], ALU.mult)

        def mix(n):
            pixels = OUT_SPANS[n]
            nc.vector.tensor_tensor(
                hid[n][:].rearrange("p (c i) t -> p c t i", i=4),
                own_and_far[:, :, pixels].rearrange("p t (c i) -> p c t i", i=4),
                near_term[:, :, pixels].rearrange("p t (c i) -> p c t i", i=4),
                ALU.subtract,
            )

        def finish(n, w3_mx):
            width = OUT_SPANS[n].stop - OUT_SPANS[n].start
            hid_mx = quantize("hid%d" % n, hid[n][:].rearrange("p c t -> p (c t)"))
            channels = bank("channels%d" % n, width, n)
            multiply(channels[:], w3_mx, slice(0, N), hid_mx, slice(0, width))
            result = tile("result%d" % n, [P, width], F32)
            nc.scalar.copy(out=result[:], in_=channels[:])
            nc.sync.dma_start(out=out[:, OUT_SPANS[n]], in_=result[:])

        near_side(LOG_SPANS[0])
        near_side(LOG_SPANS[1])
        mix(0)
        near_side(LOG_SPANS[2])
        w3_dealt = tile("w3_dealt", [P, N, PACK], BF16, tag="late")
        nc.scalar.copy(
            out=w3_dealt[:].rearrange("p (c i) j -> p c j i", i=4),
            in_=w3_raw[:].rearrange("p j (c i) -> p c j i", i=4),
        )
        w3_mx = quantize("w3", w3_dealt[:].rearrange("p n j -> p (n j)"))
        finish(0, w3_mx)
        mix(1)
        mix(2)
        finish(1, w3_mx)
        finish(2, w3_mx)
